import numpy as np
import ml_dtypes


def mxq(x, axis, fmt="e4m3"):
    dtype, down = {"e4m3": (ml_dtypes.float8_e4m3fn, 7), "e5m2": (ml_dtypes.float8_e5m2, 14)}[fmt]
    v = np.moveaxis(np.asarray(x, np.float32).astype(ml_dtypes.bfloat16).astype(np.float64), axis, -1)
    blocks = v.reshape(v.shape[:-1] + (-1, 32))
    amax = np.abs(blocks).max(-1, keepdims=True)
    byte = np.maximum(np.where(amax > 0, np.frexp(amax)[1] - 1 + 127, 0) - down, 1)
    scale = np.exp2(byte - 127.0)
    codes = (blocks / scale).astype(np.float32).astype(dtype).astype(np.float64)
    return np.moveaxis((codes * scale).reshape(v.shape), -1, axis)


WIDE = False


def mx_kscale(k):
    if not WIDE:
        return np.ones(k)
    levels = np.array([10, -10, 5, -5, 0])
    if k % 512:
        return np.exp2(np.random.permutation(np.resize(levels, k // 32))).repeat(32)
    a = np.empty((k // 512, 16))
    for p in range(k // 512):
        a[p, :8] = np.random.permutation(np.resize(levels, 8))
        for g in range(8):
            far = levels[np.abs(levels - a[p, g]) >= 10]
            a[p, g + 8] = far[np.random.randint(len(far))]
    return np.exp2(a.ravel()).repeat(32)


def f64(x):
    return np.asarray(x).astype(np.float64)


def striped(idx):
    return np.tile(np.asarray(idx).reshape(-1, 16).T, (8, 1)).astype(np.uint16)


def unstriped(offs):
    return offs[:16].T.reshape(-1).astype(np.int64)


E2M1 = np.array([0.0, 0.5, 1.0, 1.5, 2.0, 3.0, 4.0, 6.0, -0.0, -0.5, -1.0, -1.5, -2.0, -3.0, -4.0, -6.0])


def pack_weight(w, fmt):
    k, n = w.shape
    w = f64(np.asarray(w, np.float32).astype(ml_dtypes.bfloat16)).reshape(k // 32, 32, n)
    amax = np.abs(w).max(1)
    if fmt == "e4m3":
        byte = np.frexp(amax)[1] - 1 + 127 - 7
    else:
        mant, ex = np.frexp(amax / 6.0)
        byte = np.where(mant > 0.5, ex, ex - 1) + 127
    byte = np.clip(np.where(amax > 0, byte, 1), 1, 254)
    scaled = (w * np.exp2(127.0 - byte)[:, None, :]).reshape(k, n).astype(np.float32)
    by_word = np.ascontiguousarray(scaled.reshape(k // 512, 128, 4, n).transpose(0, 1, 3, 2))
    if fmt == "e4m3":
        words = by_word.astype(ml_dtypes.float8_e4m3fn).view(np.uint8)
    else:
        c = by_word.astype(ml_dtypes.float4_e2m1fn).view(np.uint8) & 0xF
        words = (c[..., 0::2] | (c[..., 1::2] << 4)).reshape(k // 512, 128, 2 * n)
    return np.ascontiguousarray(words), np.ascontiguousarray(byte.astype(np.uint8).reshape(k // 512, 16, n))


def unpack_weight(words, scales, fmt):
    g, _, n = scales.shape
    words = np.ascontiguousarray(words).reshape(g, 128, n, -1)
    if fmt == "e4m3":
        vals = words.view(ml_dtypes.float8_e4m3fn).astype(np.float64)
    else:
        nib = np.empty((g, 128, n, 4), np.uint8)
        nib[..., 0::2] = words & 0xF
        nib[..., 1::2] = words >> 4
        vals = E2M1[nib]
    vals = vals * np.repeat(np.exp2(scales.astype(np.float64) - 127.0), 8, axis=1)[..., None]
    return vals.transpose(0, 1, 3, 2).reshape(g * 512, n)


D, E, T, I, Q, G = 512, 512, 2048, 512, 128, 64


def setup_inputs():
    n = np.random.standard_normal
    idx = np.random.permutation(T)[:I]
    fd = mx_kscale(D)
    fi = mx_kscale(I)
    ti = np.ones(T)
    ti[idx] = fi
    keysp = pack_weight(n((D, T)) / fd[:, None], "e4m3")
    return {
        "query": (n((D, Q)) * 0.6 / np.sqrt(D) * fd[:, None]).astype(np.float32),
        "keys_words": keysp[0],
        "keys_scales": keysp[1],
        "pw": (np.random.uniform(0.5, 1.6, (Q, 1))).astype(np.float32),
        "os": (np.random.uniform(1.0, 4.0, (1, I)) * fi).astype(np.float32),
        "vals": (n((E, T)) / ti).astype(np.float32),
        "offs": striped(idx),
    }


def reference(query, keys_words, keys_scales, pw, os, vals, offs):
    idx = unstriped(offs)
    keysu = unpack_weight(keys_words, keys_scales, "e4m3")
    queryq = mxq(f64(query), 0, "e4m3")
    keysidxg = keysu[:, idx]
    a = queryq.T @ keysidxg
    x1 = np.exp(a)
    s = x1.reshape(Q, G, I // G).sum(axis=2)
    z = np.sum(x1, axis=1, keepdims=True)
    ls = np.log(s)
    lr = np.repeat(ls, I // G, axis=1)
    sr = np.repeat(s, I // G, axis=1)
    w = np.exp((a - lr) * f64(pw)) * sr / z
    wo1 = w * f64(os)
    wt1 = wo1.T
    vt1 = f64(vals)[:, idx].T
    wt1q = mxq(wt1, 0, "e4m3")
    vt1q = mxq(vt1, 0, "e4m3")
    o = wt1q.T @ vt1q
    return o

@@ -1,0 +1,167 @@
+from contextlib import ExitStack
+
+import concourse.mybir as mybir
+from concourse.masks import make_identity
+
+F32 = mybir.dt.float32
+BF16 = mybir.dt.bfloat16
+I32 = mybir.dt.int32
+U32 = mybir.dt.uint32
+U16 = mybir.dt.uint16
+U8 = mybir.dt.uint8
+FP8X4 = mybir.dt.float8_e4m3fn_x4
+ALU = mybir.AluOpType
+ACT = mybir.ActivationFunctionType
+AX = mybir.AxisListType
+
+P = 128
+D, E, T, I, Q, G = 512, 512, 2048, 512, 128, 64
+PAGE = I // G
+PACK = 4
+E_TILES = E // P
+LN_FLOOR = 2.0 ** -64
+
+FLOPS = 2 * Q * I * D + 2 * Q * I * E
+
+
+def tile_attend_sharedpower_kernel(tc, query, keys_words, keys_scales, pw, slot_factor, vals, offs, out):
+    nc = tc.nc
+    with ExitStack() as ctx:
+        sb = ctx.enter_context(tc.tile_pool(name="sb", bufs=1))
+        big = ctx.enter_context(tc.tile_pool(name="big", bufs=1))
+        ps = ctx.enter_context(tc.psum_pool(name="ps", bufs=1))
+
+        offsets = sb.tile([P, I // 16], U16, name="offsets")
+        key_words = sb.tile([P, T], U32, name="key_words")
+        key_bytes = sb.tile([P, T], U8, name="key_bytes")
+        q_raw = sb.tile([P, PACK, Q], F32, name="q_raw")
+        power = sb.tile([P, 1], F32, name="power")
+        factor_cols = sb.tile([P, PACK], F32, name="factor_cols")
+        zeros = big.tile([P, E_TILES * T], F32, name="zeros", offset=0)
+        val_pool = [big.tile([P, T], F32, name=f"val_pool{j}", offset=4 * T * j) for j in range(E_TILES)]
+        ident = sb.tile([P, P], F32, name="ident")
+
+        nc.vector.memset(key_bytes[:].bitcast(I32), 0)
+        nc.vector.memset(zeros[:, 0:P], 0.0)
+        nc.gpsimd.affine_select(out=ident[:], in_=zeros[:, 0:P], compare_op=ALU.not_equal, fill=1.0, base=0,
+                                pattern=[[-1, P]], channel_multiplier=1)
+        nc.sync.dma_start(key_words[:].bitcast(I32), keys_words[0].rearrange("p n t -> p (n t)").bitcast(I32))
+        nc.sync.dma_start(offsets[:], offs)
+        nc.sync.dma_start(q_raw[:], query.rearrange("(p j) q -> p j q", j=PACK))
+        for quad in range(4):
+            nc.scalar.dma_start(
+                key_bytes[32 * quad : 32 * quad + 4, :].bitcast(I32),
+                keys_scales[0, 4 * quad : 4 * quad + 4, :].bitcast(I32),
+            )
+        for j in range(E_TILES):
+            nc.sync.dma_start(val_pool[j][:], vals[j * P : (j + 1) * P, :])
+        nc.gpsimd.dma_start(power[:], pw)
+        nc.gpsimd.dma_start(factor_cols[:], slot_factor[0].rearrange("(p t) -> p t", t=PACK))
+
+        k_bytes = sb.tile([P, I], U8, name="k_bytes", align_bytes=64)
+        k_words = sb.tile([P, I], U32, name="k_words", align_bytes=64)
+        nc.vector.tensor_copy(k_bytes[:], key_bytes[:].indirect(offsets[:]))
+        nc.vector.tensor_copy(k_words[:], key_words[:].indirect(offsets[:]))
+
+        q_grouped = sb.tile([P, Q * PACK], BF16, name="q_grouped", align_bytes=64)
+        nc.scalar.copy(q_grouped[:].rearrange("p (q j) -> p q j", j=PACK), q_raw[:].rearrange("p j q -> p q j"))
+        q_words = sb.tile([P, Q], U32, name="q_words", align_bytes=64)
+        q_bytes = sb.tile([P, Q], U8, name="q_bytes", align_bytes=64)
+        nc.vector.quantize_mx(q_words[:].bitcast(FP8X4), q_bytes[:], q_grouped[:])
+
+        scores = ps.tile([P, I], F32, name="scores")
+        nc.tensor.matmul_mx(scores[:], lhsT=q_words[:].bitcast(FP8X4), lhsT_scale=q_bytes[:],
+                            rhs=k_words[:].bitcast(FP8X4), rhs_scale=k_bytes[:], start=True, stop=True)
+
+        factor_rows = ps.tile([P, PACK, P], F32, name="factor_rows")
+        for t in range(PACK):
+            nc.tensor.transpose(factor_rows[:, t, :], factor_cols[:, t : t + 1].to_broadcast([P, P]), ident[:])
+
+        one_less_power = sb.tile([P, 1], F32, name="one_less_power")
+        nc.vector.tensor_scalar(one_less_power[:], power[:], -1.0, 1.0, ALU.mult, ALU.add)
+
+        neg_max = sb.tile([P, 1], F32, name="neg_max")
+        nc.vector.tensor_reduce(neg_max[:], scores[:], AX.X, ALU.max, negate=True)
+        exps = sb.tile([P, I], F32, name="exps")
+        sums = sb.tile([P, G + 1], F32, name="sums")
+        nc.scalar.activation(exps[:], scores[:], ACT.Exp, bias=neg_max[:], scale=1.0, accum_out=sums[:, G : G + 1])
+        neg_max_power = sb.tile([P, 1], F32, name="neg_max_power")
+        nc.vector.tensor_tensor(neg_max_power[:], neg_max[:], power[:], ALU.mult)
+
+        v_listed = [sb.tile([P, I], BF16, name=f"v_listed{j}") for j in range(E_TILES)]
+
+        def on_pool(j, at, shape, dtype, name):
+            return big.tile(shape, dtype, name=name, offset=4 * T * j + at, align_bytes=64)
+
+        def turn(listed, grouped, tag, bufs):
+            pairs = listed[:].bitcast(F32)
+            turned = ps.tile([P, 2, P], F32, name="turned", tag=tag, bufs=bufs)
+            for u in range(2):
+                nc.tensor.transpose(turned[:, u, :], pairs[:, u * P : (u + 1) * P], ident[:])
+            nc.scalar.copy(grouped.bitcast(F32).rearrange("p (r u) -> p r u", u=2), turned[:].rearrange("p u r -> p r u"))
+
+        def gather_vals(j):
+            nc.vector.tensor_copy(v_listed[j][:].rearrange("p (u b y) -> p b u y", u=2, y=16), val_pool[j][:].indirect(offsets[:]))
+
+        def quantise(words, scale_bytes, grouped):
+            nc.vector.quantize_mx(words[:].bitcast(FP8X4), scale_bytes[:], grouped[:])
+
+        nc.vector.tensor_reduce(sums[:, 0:G], exps[:].rearrange("p (g s) -> p g s", s=PAGE), AX.X, ALU.add)
+        gather_vals(0)
+        logs = sb.tile([P, G + 1], F32, name="logs")
+        nc.scalar.activation(logs[:], sums[:], ACT.Ln, bias=LN_FLOOR, scale=1.0)
+        page_term = on_pool(0, 0, [P, G], F32, "page_term")
+        nc.vector.tensor_scalar(page_term[:], logs[:, 0:G], one_less_power[:], None, ALU.mult)
+        row_term = on_pool(0, 256, [P, 1], F32, "row_term")
+        nc.vector.tensor_tensor(row_term[:], neg_max_power[:], logs[:, G : G + 1], ALU.subtract)
+        exponent = sb.tile([P, I], F32, name="exponent", tag="shared", align_bytes=64)
+        nc.vector.scalar_tensor_tensor(
+            exponent[:].rearrange("p (g s) -> p g s", s=PAGE),
+            scores[:].rearrange("p (g s) -> p g s", s=PAGE),
+            power[:],
+            page_term[:].unsqueeze(2).to_broadcast([P, G, PAGE]),
+            ALU.mult, ALU.add)
+        gather_vals(1)
+        shares = sb.tile([P, I], F32, name="shares")
+        nc.scalar.activation(shares[:], exponent[:], ACT.Exp, bias=row_term[:], scale=1.0)
+        grouped01 = sb.tile([P, 2 * I], BF16, name="grouped01", tag="shared", align_bytes=64)
+        turn(v_listed[0], grouped01[:, 0:I], "v_turned", 2)
+        turn(v_listed[1], grouped01[:, I : 2 * I], "v_turned", 2)
+        weights = on_pool(1, 0, [P, I], BF16, "weights")
+        nc.vector.tensor_tensor(
+            weights[:].rearrange("p (u b n t) -> p b u n t", u=2, n=4, t=PACK),
+            shares[:].rearrange("p (b u n t) -> p b u n t", u=2, n=4, t=PACK),
+            factor_rows[:].rearrange("p t (b u n) -> p b u n t", u=2, n=4),
+            ALU.mult)
+        gather_vals(2)
+        w_grouped = sb.tile([P, I], BF16, name="w_grouped", align_bytes=64)
+        turn(weights, w_grouped[:], "w_turned", 1)
+        grouped2 = sb.tile([P, I], BF16, name="grouped2", align_bytes=64)
+        turn(v_listed[2], grouped2[:], "v_turned", 2)
+        words01 = on_pool(2, 0, [P, 2 * P], U32, "words01")
+        bytes01 = on_pool(2, 1024, [P, 2 * P], U8, "bytes01")
+        quantise(words01, bytes01, grouped01)
+        w_words = on_pool(2, 2048, [P, Q], U32, "w_words")
+        w_bytes = on_pool(2, 3072, [P, Q], U8, "w_bytes")
+        quantise(w_words, w_bytes, w_grouped)
+        gather_vals(3)
+
+        def product(words, scale_bytes, col, width, copy):
+            bank = ps.tile([P, width], F32, name=f"bank{col}")
+            nc.tensor.matmul_mx(bank[:], lhsT=w_words[:].bitcast(FP8X4), lhsT_scale=w_bytes[:],
+                                rhs=words[:].bitcast(FP8X4), rhs_scale=scale_bytes[:], start=True, stop=True)
+            staged = sb.tile([P, width], F32, name=f"staged{col}")
+            copy(staged[:], bank[:])
+            nc.sync.dma_start(out[:, col : col + width], staged[:])
+
+        product(words01, bytes01, 0, 2 * P, nc.scalar.copy)
+        grouped3 = sb.tile([P, I], BF16, name="grouped3", align_bytes=64)
+        turn(v_listed[3], grouped3[:], "v_turned", 2)
+        words2 = on_pool(3, 0, [P, P], U32, "words2")
+        bytes2 = on_pool(3, 1024, [P, P], U8, "bytes2")
+        quantise(words2, bytes2, grouped2)
+        product(words2, bytes2, 2 * P, P, nc.scalar.copy)
+        words3 = sb.tile([P, P], U32, name="words3", align_bytes=64)
+        bytes3 = sb.tile([P, P], U8, name="bytes3", align_bytes=64)
+        quantise(words3, bytes3, grouped3)
+        product(words3, bytes3, 3 * P, P, nc.vector.tensor_copy)

@@ -32,31 +32,38 @@ def tile_attend_sharedpower_kernel(tc, query, keys_words, keys_scales, pw, slot_
         ps = ctx.enter_context(tc.psum_pool(name="ps", bufs=1))
 
         offsets = sb.tile([P, I // 16], U16, name="offsets")
-        key_words = sb.tile([P, T], U32, name="key_words")
         key_bytes = sb.tile([P, T], U8, name="key_bytes")
         q_raw = sb.tile([P, PACK, Q], F32, name="q_raw")
-        power = sb.tile([P, 1], F32, name="power")
-        factor_cols = sb.tile([P, PACK], F32, name="factor_cols")
-        zeros = big.tile([P, E_TILES * T], F32, name="zeros", offset=0)
-        val_pool = [big.tile([P, T], F32, name=f"val_pool{j}", offset=4 * T * j) for j in range(E_TILES)]
+        zeros = [
+            big.tile([P, T], F32, name="zeros0", offset=0),
+            big.tile([P, E_TILES * T + 16], F32, name="zeros1", offset=4 * T),
+        ]
+        power = big.tile([P, 1], F32, name="power", offset=4 * T * (E_TILES + 1))
+        factor_cols = big.tile([P, PACK], F32, name="factor_cols", offset=4 * T * (E_TILES + 1) + 32)
+        key_words = big.tile([P, T], U32, name="key_words", offset=0)
+        val_pool = [big.tile([P, T], F32, name=f"val_pool{j}", offset=4 * T * (j + 1)) for j in range(E_TILES)]
         ident = sb.tile([P, P], F32, name="ident")
 
         nc.vector.memset(key_bytes[:].bitcast(I32), 0)
-        nc.vector.memset(zeros[:, 0:P], 0.0)
-        nc.gpsimd.affine_select(out=ident[:], in_=zeros[:, 0:P], compare_op=ALU.not_equal, fill=1.0, base=0,
-                                pattern=[[-1, P]], channel_multiplier=1)
-        nc.sync.dma_start(key_words[:].bitcast(I32), keys_words[0].rearrange("p n t -> p (n t)").bitcast(I32))
+        half = P // 2
+        for h in range(2):
+            nc.gpsimd.memset(zeros[h][:, 0:half], 0.0)
+            nc.gpsimd.affine_select(out=ident[:, h * half : (h + 1) * half], in_=zeros[h][:, 0:half],
+                                    compare_op=ALU.not_equal, fill=1.0, base=-h * half,
+                                    pattern=[[-1, half]], channel_multiplier=1)
         nc.sync.dma_start(offsets[:], offs)
         nc.sync.dma_start(q_raw[:], query.rearrange("(p j) q -> p j q", j=PACK))
         for quad in range(4):
-            nc.scalar.dma_start(
+            nc.sync.dma_start(
                 key_bytes[32 * quad : 32 * quad + 4, :].bitcast(I32),
                 keys_scales[0, 4 * quad : 4 * quad + 4, :].bitcast(I32),
             )
-        for j in range(E_TILES):
+        nc.sync.dma_start(key_words[:].bitcast(I32), keys_words[0].rearrange("p n t -> p (n t)").bitcast(I32))
+        nc.sync.dma_start(val_pool[0][:], vals[0:P, :])
+        nc.sync.dma_start(power[:], pw)
+        nc.sync.dma_start(factor_cols[:], slot_factor[0].rearrange("(p t) -> p t", t=PACK))
+        for j in range(1, E_TILES):
             nc.sync.dma_start(val_pool[j][:], vals[j * P : (j + 1) * P, :])
-        nc.gpsimd.dma_start(power[:], pw)
-        nc.gpsimd.dma_start(factor_cols[:], slot_factor[0].rearrange("(p t) -> p t", t=PACK))
 
         k_bytes = sb.tile([P, I], U8, name="k_bytes", align_bytes=64)
         k_words = sb.tile([P, I], U32, name="k_words", align_bytes=64)
@@ -77,21 +84,18 @@ def tile_attend_sharedpower_kernel(tc, query, keys_words, keys_scales, pw, slot_
         for t in range(PACK):
             nc.tensor.transpose(factor_rows[:, t, :], factor_cols[:, t : t + 1].to_broadcast([P, P]), ident[:])
 
-        one_less_power = sb.tile([P, 1], F32, name="one_less_power")
-        nc.vector.tensor_scalar(one_less_power[:], power[:], -1.0, 1.0, ALU.mult, ALU.add)
-
         neg_max = sb.tile([P, 1], F32, name="neg_max")
         nc.vector.tensor_reduce(neg_max[:], scores[:], AX.X, ALU.max, negate=True)
+        row_sum = sb.tile([P, 1], F32, name="row_sum")
         exps = sb.tile([P, I], F32, name="exps")
-        sums = sb.tile([P, G + 1], F32, name="sums")
-        nc.scalar.activation(exps[:], scores[:], ACT.Exp, bias=neg_max[:], scale=1.0, accum_out=sums[:, G : G + 1])
-        neg_max_power = sb.tile([P, 1], F32, name="neg_max_power")
-        nc.vector.tensor_tensor(neg_max_power[:], neg_max[:], power[:], ALU.mult)
+        nc.scalar.activation(exps[:], scores[:], ACT.Exp, bias=neg_max[:], scale=1.0, accum_out=row_sum[:])
+        row_log = sb.tile([P, 1], F32, name="row_log")
+        nc.scalar.activation(row_log[:], row_sum[:], ACT.Ln)
 
         v_listed = [sb.tile([P, I], BF16, name=f"v_listed{j}") for j in range(E_TILES)]
 
         def on_pool(j, at, shape, dtype, name):
-            return big.tile(shape, dtype, name=name, offset=4 * T * j + at, align_bytes=64)
+            return big.tile(shape, dtype, name=name, offset=4 * T * (j + 1) + at, align_bytes=64)
 
         def turn(listed, grouped, tag, bufs):
             pairs = listed[:].bitcast(F32)
@@ -106,14 +110,20 @@ def tile_attend_sharedpower_kernel(tc, query, keys_words, keys_scales, pw, slot_
         def quantise(words, scale_bytes, grouped):
             nc.vector.quantize_mx(words[:].bitcast(FP8X4), scale_bytes[:], grouped[:])
 
-        nc.vector.tensor_reduce(sums[:, 0:G], exps[:].rearrange("p (g s) -> p g s", s=PAGE), AX.X, ALU.add)
         gather_vals(0)
-        logs = sb.tile([P, G + 1], F32, name="logs")
+        sums = on_pool(0, 0, [P, G], F32, "sums")
+        nc.vector.tensor_reduce(sums[:], exps[:].rearrange("p (g s) -> p g s", s=PAGE), AX.X, ALU.add)
+        one_less_power = on_pool(0, 512, [P, 1], F32, "one_less_power")
+        nc.vector.tensor_scalar(one_less_power[:], power[:], -1.0, 1.0, ALU.mult, ALU.add)
+        neg_max_power = on_pool(0, 576, [P, 1], F32, "neg_max_power")
+        nc.vector.tensor_tensor(neg_max_power[:], neg_max[:], power[:], ALU.mult)
+        gather_vals(1)
+        logs = sb.tile([P, G], F32, name="logs")
         nc.scalar.activation(logs[:], sums[:], ACT.Ln, bias=LN_FLOOR, scale=1.0)
-        page_term = on_pool(0, 0, [P, G], F32, "page_term")
-        nc.vector.tensor_scalar(page_term[:], logs[:, 0:G], one_less_power[:], None, ALU.mult)
-        row_term = on_pool(0, 256, [P, 1], F32, "row_term")
-        nc.vector.tensor_tensor(row_term[:], neg_max_power[:], logs[:, G : G + 1], ALU.subtract)
+        page_term = on_pool(1, 0, [P, G], F32, "page_term")
+        nc.vector.tensor_scalar(page_term[:], logs[:], one_less_power[:], None, ALU.mult)
+        row_term = on_pool(1, 256, [P, 1], F32, "row_term")
+        nc.vector.tensor_tensor(row_term[:], neg_max_power[:], row_log[:], ALU.subtract)
         exponent = sb.tile([P, I], F32, name="exponent", tag="shared", align_bytes=64)
         nc.vector.scalar_tensor_tensor(
             exponent[:].rearrange("p (g s) -> p g s", s=PAGE),
@@ -121,47 +131,51 @@ def tile_attend_sharedpower_kernel(tc, query, keys_words, keys_scales, pw, slot_
             power[:],
             page_term[:].unsqueeze(2).to_broadcast([P, G, PAGE]),
             ALU.mult, ALU.add)
-        gather_vals(1)
+        gather_vals(2)
         shares = sb.tile([P, I], F32, name="shares")
         nc.scalar.activation(shares[:], exponent[:], ACT.Exp, bias=row_term[:], scale=1.0)
         grouped01 = sb.tile([P, 2 * I], BF16, name="grouped01", tag="shared", align_bytes=64)
         turn(v_listed[0], grouped01[:, 0:I], "v_turned", 2)
         turn(v_listed[1], grouped01[:, I : 2 * I], "v_turned", 2)
-        weights = on_pool(1, 0, [P, I], BF16, "weights")
+        weights = on_pool(2, 4096, [P, I], BF16, "weights")
         nc.vector.tensor_tensor(
             weights[:].rearrange("p (u b n t) -> p b u n t", u=2, n=4, t=PACK),
             shares[:].rearrange("p (b u n t) -> p b u n t", u=2, n=4, t=PACK),
             factor_rows[:].rearrange("p t (b u n) -> p b u n t", u=2, n=4),
             ALU.mult)
-        gather_vals(2)
-        w_grouped = sb.tile([P, I], BF16, name="w_grouped", align_bytes=64)
-        turn(weights, w_grouped[:], "w_turned", 1)
         grouped2 = sb.tile([P, I], BF16, name="grouped2", align_bytes=64)
         turn(v_listed[2], grouped2[:], "v_turned", 2)
-        words01 = on_pool(2, 0, [P, 2 * P], U32, "words01")
-        bytes01 = on_pool(2, 1024, [P, 2 * P], U8, "bytes01")
-        quantise(words01, bytes01, grouped01)
-        w_words = on_pool(2, 2048, [P, Q], U32, "w_words")
-        w_bytes = on_pool(2, 3072, [P, Q], U8, "w_bytes")
-        quantise(w_words, w_bytes, w_grouped)
+        w_grouped = sb.tile([P, I], BF16, name="w_grouped", align_bytes=64)
+        turn(weights, w_grouped[:], "w_turned", 1)
         gather_vals(3)
-
-        def product(words, scale_bytes, col, width, copy):
-            bank = ps.tile([P, width], F32, name=f"bank{col}")
-            nc.tensor.matmul_mx(bank[:], lhsT=w_words[:].bitcast(FP8X4), lhsT_scale=w_bytes[:],
-                                rhs=words[:].bitcast(FP8X4), rhs_scale=scale_bytes[:], start=True, stop=True)
-            staged = sb.tile([P, width], F32, name=f"staged{col}")
-            copy(staged[:], bank[:])
-            nc.sync.dma_start(out[:, col : col + width], staged[:])
-
-        product(words01, bytes01, 0, 2 * P, nc.scalar.copy)
         grouped3 = sb.tile([P, I], BF16, name="grouped3", align_bytes=64)
         turn(v_listed[3], grouped3[:], "v_turned", 2)
-        words2 = on_pool(3, 0, [P, P], U32, "words2")
-        bytes2 = on_pool(3, 1024, [P, P], U8, "bytes2")
+        w_words = on_pool(3, 2048, [P, Q], U32, "w_words")
+        w_bytes = on_pool(3, 3072, [P, Q], U8, "w_bytes")
+        quantise(w_words, w_bytes, w_grouped)
+        words01 = on_pool(3, 0, [P, 2 * P], U32, "words01")
+        bytes01 = on_pool(3, 1024, [P, 2 * P], U8, "bytes01")
+        quantise(words01, bytes01, grouped01)
+        words2 = on_pool(3, 4096, [P, P], U32, "words2")
+        bytes2 = on_pool(3, 5120, [P, P], U8, "bytes2")
         quantise(words2, bytes2, grouped2)
-        product(words2, bytes2, 2 * P, P, nc.scalar.copy)
+
+        def product(bank, words, scale_bytes):
+            nc.tensor.matmul_mx(bank, lhsT=w_words[:].bitcast(FP8X4), lhsT_scale=w_bytes[:],
+                                rhs=words[:].bitcast(FP8X4), rhs_scale=scale_bytes[:], start=True, stop=True)
+
+        early = ps.tile([P, 3 * P], F32, name="early")
+        product(early[:, 0 : 2 * P], words01, bytes01)
+        product(early[:, 2 * P : 3 * P], words2, bytes2)
+        early_sb = sb.tile([P, 3 * P], F32, name="early_sb")
+        nc.scalar.copy(early_sb[:], early[:])
+        nc.sync.dma_start(out[:, 0 : 3 * P], early_sb[:])
+
         words3 = sb.tile([P, P], U32, name="words3", align_bytes=64)
         bytes3 = sb.tile([P, P], U8, name="bytes3", align_bytes=64)
         quantise(words3, bytes3, grouped3)
-        product(words3, bytes3, 3 * P, P, nc.vector.tensor_copy)
+        last = ps.tile([P, P], F32, name="last")
+        product(last[:], words3, bytes3)
+        last_sb = sb.tile([P, P], F32, name="last_sb")
+        nc.vector.tensor_copy(last_sb[:], last[:])
+        nc.sync.dma_start(out[:, 3 * P : 4 * P], last_sb[:])

@@ -1,7 +1,6 @@
 from contextlib import ExitStack
 
 import concourse.mybir as mybir
-from concourse.masks import make_identity
 
 F32 = mybir.dt.float32
 BF16 = mybir.dt.bfloat16
@@ -18,8 +17,11 @@ P = 128
 D, E, T, I, Q, G = 512, 512, 2048, 512, 128, 64
 PAGE = I // G
 PACK = 4
+QUADRANTS = 4
 E_TILES = E // P
-LN_FLOOR = 2.0 ** -64
+POOL_BYTES = 4 * T
+RUN = 16
+LN_FLOOR = 2.0**-64
 
 FLOPS = 2 * Q * I * D + 2 * Q * I * E
 
@@ -28,57 +30,83 @@ def tile_attend_sharedpower_kernel(tc, query, keys_words, keys_scales, pw, slot_
     nc = tc.nc
     with ExitStack() as ctx:
         sb = ctx.enter_context(tc.tile_pool(name="sb", bufs=1))
-        big = ctx.enter_context(tc.tile_pool(name="big", bufs=1))
+        placed = ctx.enter_context(tc.tile_pool(name="placed", bufs=1))
         ps = ctx.enter_context(tc.psum_pool(name="ps", bufs=1))
 
+        vectors_at = (1 + E_TILES) * POOL_BYTES
         offsets = sb.tile([P, I // 16], U16, name="offsets")
         key_bytes = sb.tile([P, T], U8, name="key_bytes")
         q_raw = sb.tile([P, PACK, Q], F32, name="q_raw")
         zeros = [
-            big.tile([P, T], F32, name="zeros0", offset=0),
-            big.tile([P, E_TILES * T + 16], F32, name="zeros1", offset=4 * T),
+            placed.tile([P, T], F32, name="zeros0", offset=0),
+            placed.tile([P, E_TILES * T + 16], F32, name="zeros1", offset=POOL_BYTES),
         ]
-        power = big.tile([P, 1], F32, name="power", offset=4 * T * (E_TILES + 1))
-        factor_cols = big.tile([P, PACK], F32, name="factor_cols", offset=4 * T * (E_TILES + 1) + 32)
-        key_words = big.tile([P, T], U32, name="key_words", offset=0)
-        val_pool = [big.tile([P, T], F32, name=f"val_pool{j}", offset=4 * T * (j + 1)) for j in range(E_TILES)]
+        power = placed.tile([P, 1], F32, name="power", offset=vectors_at)
+        factor_cols = placed.tile([P, PACK], F32, name="factor_cols", offset=vectors_at + 32)
+        key_words = placed.tile([P, T], U32, name="key_words", offset=0)
+        val_pool = [placed.tile([P, T], F32, name=f"val_pool{j}", offset=(1 + j) * POOL_BYTES) for j in range(E_TILES)]
         ident = sb.tile([P, P], F32, name="ident")
+
+        def after_gather(j, at, shape, dtype, name):
+            return placed.tile(shape, dtype, name=name, offset=(1 + j) * POOL_BYTES + at, align_bytes=64)
+
+        def load_vals(j):
+            nc.sync.dma_start(val_pool[j][:], vals[j * P : (j + 1) * P, :])
 
         nc.vector.memset(key_bytes[:].bitcast(I32), 0)
         half = P // 2
         for h in range(2):
             nc.gpsimd.memset(zeros[h][:, 0:half], 0.0)
-            nc.gpsimd.affine_select(out=ident[:, h * half : (h + 1) * half], in_=zeros[h][:, 0:half],
-                                    compare_op=ALU.not_equal, fill=1.0, base=-h * half,
-                                    pattern=[[-1, half]], channel_multiplier=1)
+            nc.gpsimd.affine_select(
+                out=ident[:, h * half : (h + 1) * half],
+                in_=zeros[h][:, 0:half],
+                compare_op=ALU.not_equal,
+                fill=1.0,
+                base=-h * half,
+                pattern=[[-1, half]],
+                channel_multiplier=1,
+            )
+
         nc.sync.dma_start(offsets[:], offs)
         nc.sync.dma_start(q_raw[:], query.rearrange("(p j) q -> p j q", j=PACK))
-        for quad in range(4):
-            nc.sync.dma_start(
+        for quad in range(QUADRANTS):
+            queue = nc.sync if quad % 2 == 0 else nc.scalar
+            queue.dma_start(
                 key_bytes[32 * quad : 32 * quad + 4, :].bitcast(I32),
                 keys_scales[0, 4 * quad : 4 * quad + 4, :].bitcast(I32),
             )
         nc.sync.dma_start(key_words[:].bitcast(I32), keys_words[0].rearrange("p n t -> p (n t)").bitcast(I32))
-        nc.sync.dma_start(val_pool[0][:], vals[0:P, :])
+        load_vals(0)
         nc.sync.dma_start(power[:], pw)
         nc.sync.dma_start(factor_cols[:], slot_factor[0].rearrange("(p t) -> p t", t=PACK))
         for j in range(1, E_TILES):
-            nc.sync.dma_start(val_pool[j][:], vals[j * P : (j + 1) * P, :])
+            load_vals(j)
+
+        def quantise(words, scale_bytes, grouped):
+            nc.vector.quantize_mx(words[:].bitcast(FP8X4), scale_bytes[:], grouped[:])
 
         k_bytes = sb.tile([P, I], U8, name="k_bytes", align_bytes=64)
         k_words = sb.tile([P, I], U32, name="k_words", align_bytes=64)
         nc.vector.tensor_copy(k_bytes[:], key_bytes[:].indirect(offsets[:]))
-        nc.vector.tensor_copy(k_words[:], key_words[:].indirect(offsets[:]))
-
         q_grouped = sb.tile([P, Q * PACK], BF16, name="q_grouped", align_bytes=64)
         nc.scalar.copy(q_grouped[:].rearrange("p (q j) -> p q j", j=PACK), q_raw[:].rearrange("p j q -> p q j"))
         q_words = sb.tile([P, Q], U32, name="q_words", align_bytes=64)
         q_bytes = sb.tile([P, Q], U8, name="q_bytes", align_bytes=64)
-        nc.vector.quantize_mx(q_words[:].bitcast(FP8X4), q_bytes[:], q_grouped[:])
-
+        quantise(q_words, q_bytes, q_grouped)
         scores = ps.tile([P, I], F32, name="scores")
-        nc.tensor.matmul_mx(scores[:], lhsT=q_words[:].bitcast(FP8X4), lhsT_scale=q_bytes[:],
-                            rhs=k_words[:].bitcast(FP8X4), rhs_scale=k_bytes[:], start=True, stop=True)
+        for h in range(2):
+            slots = slice(h * I // 2, (h + 1) * I // 2)
+            listed = offsets[:, slots.start // 16 : slots.stop // 16]
+            nc.vector.tensor_copy(k_words[:, slots], key_words[:].indirect(listed))
+            nc.tensor.matmul_mx(
+                scores[:, slots],
+                lhsT=q_words[:].bitcast(FP8X4),
+                lhsT_scale=q_bytes[:],
+                rhs=k_words[:, slots].bitcast(FP8X4),
+                rhs_scale=k_bytes[:, slots],
+                start=True,
+                stop=True,
+            )
 
         factor_rows = ps.tile([P, PACK, P], F32, name="factor_rows")
         for t in range(PACK):
@@ -92,90 +120,97 @@ def tile_attend_sharedpower_kernel(tc, query, keys_words, keys_scales, pw, slot_
         row_log = sb.tile([P, 1], F32, name="row_log")
         nc.scalar.activation(row_log[:], row_sum[:], ACT.Ln)
 
-        v_listed = [sb.tile([P, I], BF16, name=f"v_listed{j}") for j in range(E_TILES)]
+        v_dealt = [sb.tile([P, I], BF16, name=f"v_dealt{j}") for j in range(E_TILES)]
 
-        def on_pool(j, at, shape, dtype, name):
-            return big.tile(shape, dtype, name=name, offset=4 * T * (j + 1) + at, align_bytes=64)
+        def gather_vals(j):
+            nc.vector.tensor_copy(
+                v_dealt[j][:].rearrange("p (u b y) -> p b u y", u=2, y=RUN), val_pool[j][:].indirect(offsets[:])
+            )
 
-        def turn(listed, grouped, tag, bufs):
-            pairs = listed[:].bitcast(F32)
+        def turn(dealt, grouped, tag, bufs):
+            pairs = dealt[:].bitcast(F32)
             turned = ps.tile([P, 2, P], F32, name="turned", tag=tag, bufs=bufs)
             for u in range(2):
                 nc.tensor.transpose(turned[:, u, :], pairs[:, u * P : (u + 1) * P], ident[:])
-            nc.scalar.copy(grouped.bitcast(F32).rearrange("p (r u) -> p r u", u=2), turned[:].rearrange("p u r -> p r u"))
+            nc.scalar.copy(grouped.bitcast(F32).rearrange("p (c u) -> p c u", u=2), turned[:].rearrange("p u c -> p c u"))
 
-        def gather_vals(j):
-            nc.vector.tensor_copy(v_listed[j][:].rearrange("p (u b y) -> p b u y", u=2, y=16), val_pool[j][:].indirect(offsets[:]))
-
-        def quantise(words, scale_bytes, grouped):
-            nc.vector.quantize_mx(words[:].bitcast(FP8X4), scale_bytes[:], grouped[:])
+        def turn_vals(j, grouped):
+            turn(v_dealt[j], grouped, "v_turned", 2)
 
         gather_vals(0)
-        sums = on_pool(0, 0, [P, G], F32, "sums")
-        nc.vector.tensor_reduce(sums[:], exps[:].rearrange("p (g s) -> p g s", s=PAGE), AX.X, ALU.add)
-        one_less_power = on_pool(0, 512, [P, 1], F32, "one_less_power")
+        page_sum = after_gather(0, 0, [P, G], F32, "page_sum")
+        nc.vector.tensor_reduce(page_sum[:], exps[:].rearrange("p (g s) -> p g s", s=PAGE), AX.X, ALU.add)
+        one_less_power = after_gather(0, 512, [P, 1], F32, "one_less_power")
         nc.vector.tensor_scalar(one_less_power[:], power[:], -1.0, 1.0, ALU.mult, ALU.add)
-        neg_max_power = on_pool(0, 576, [P, 1], F32, "neg_max_power")
+        neg_max_power = after_gather(0, 576, [P, 1], F32, "neg_max_power")
         nc.vector.tensor_tensor(neg_max_power[:], neg_max[:], power[:], ALU.mult)
+
         gather_vals(1)
-        logs = sb.tile([P, G], F32, name="logs")
-        nc.scalar.activation(logs[:], sums[:], ACT.Ln, bias=LN_FLOOR, scale=1.0)
-        page_term = on_pool(1, 0, [P, G], F32, "page_term")
-        nc.vector.tensor_scalar(page_term[:], logs[:], one_less_power[:], None, ALU.mult)
-        row_term = on_pool(1, 256, [P, 1], F32, "row_term")
+        page_log = sb.tile([P, G], F32, name="page_log")
+        nc.scalar.activation(page_log[:], page_sum[:], ACT.Ln, bias=LN_FLOOR, scale=1.0)
+        page_term = after_gather(1, 0, [P, G], F32, "page_term")
+        nc.vector.tensor_scalar(page_term[:], page_log[:], one_less_power[:], None, ALU.mult)
+        row_term = after_gather(1, 256, [P, 1], F32, "row_term")
         nc.vector.tensor_tensor(row_term[:], neg_max_power[:], row_log[:], ALU.subtract)
-        exponent = sb.tile([P, I], F32, name="exponent", tag="shared", align_bytes=64)
+        exponent = sb.tile([P, I], F32, name="exponent", tag="exponent_bytes", align_bytes=64)
         nc.vector.scalar_tensor_tensor(
             exponent[:].rearrange("p (g s) -> p g s", s=PAGE),
             scores[:].rearrange("p (g s) -> p g s", s=PAGE),
             power[:],
             page_term[:].unsqueeze(2).to_broadcast([P, G, PAGE]),
-            ALU.mult, ALU.add)
+            ALU.mult,
+            ALU.add,
+        )
+
         gather_vals(2)
         shares = sb.tile([P, I], F32, name="shares")
         nc.scalar.activation(shares[:], exponent[:], ACT.Exp, bias=row_term[:], scale=1.0)
-        grouped01 = sb.tile([P, 2 * I], BF16, name="grouped01", tag="shared", align_bytes=64)
-        turn(v_listed[0], grouped01[:, 0:I], "v_turned", 2)
-        turn(v_listed[1], grouped01[:, I : 2 * I], "v_turned", 2)
-        weights = on_pool(2, 4096, [P, I], BF16, "weights")
+        grouped01 = sb.tile([P, 2 * I], BF16, name="grouped01", tag="exponent_bytes", align_bytes=64)
+        turn_vals(0, grouped01[:, 0:I])
+        turn_vals(1, grouped01[:, I : 2 * I])
+        weights = after_gather(2, 4096, [P, I], BF16, "weights")
         nc.vector.tensor_tensor(
-            weights[:].rearrange("p (u b n t) -> p b u n t", u=2, n=4, t=PACK),
-            shares[:].rearrange("p (b u n t) -> p b u n t", u=2, n=4, t=PACK),
-            factor_rows[:].rearrange("p t (b u n) -> p b u n t", u=2, n=4),
-            ALU.mult)
+            weights[:].rearrange("p (u b n t) -> p b u n t", u=2, n=RUN // PACK, t=PACK),
+            shares[:].rearrange("p (b u n t) -> p b u n t", u=2, n=RUN // PACK, t=PACK),
+            factor_rows[:].rearrange("p t (b u n) -> p b u n t", u=2, n=RUN // PACK),
+            ALU.mult,
+        )
         grouped2 = sb.tile([P, I], BF16, name="grouped2", align_bytes=64)
-        turn(v_listed[2], grouped2[:], "v_turned", 2)
+        turn_vals(2, grouped2[:])
         w_grouped = sb.tile([P, I], BF16, name="w_grouped", align_bytes=64)
         turn(weights, w_grouped[:], "w_turned", 1)
+
         gather_vals(3)
         grouped3 = sb.tile([P, I], BF16, name="grouped3", align_bytes=64)
-        turn(v_listed[3], grouped3[:], "v_turned", 2)
-        w_words = on_pool(3, 2048, [P, Q], U32, "w_words")
-        w_bytes = on_pool(3, 3072, [P, Q], U8, "w_bytes")
+        turn_vals(3, grouped3[:])
+        w_words = after_gather(3, 2048, [P, Q], U32, "w_words")
+        w_bytes = after_gather(3, 3072, [P, Q], U8, "w_bytes")
         quantise(w_words, w_bytes, w_grouped)
-        words01 = on_pool(3, 0, [P, 2 * P], U32, "words01")
-        bytes01 = on_pool(3, 1024, [P, 2 * P], U8, "bytes01")
+
+        def product(words, scale_bytes, first, width, copy):
+            bank = ps.tile([P, width], F32, name=f"bank{first}")
+            nc.tensor.matmul_mx(
+                bank[:],
+                lhsT=w_words[:].bitcast(FP8X4),
+                lhsT_scale=w_bytes[:],
+                rhs=words[:].bitcast(FP8X4),
+                rhs_scale=scale_bytes[:],
+                start=True,
+                stop=True,
+            )
+            staged = sb.tile([P, width], F32, name=f"staged{first}")
+            copy(staged[:], bank[:])
+            nc.sync.dma_start(out[:, first : first + width], staged[:])
+
+        words01 = after_gather(3, 0, [P, 2 * P], U32, "words01")
+        bytes01 = after_gather(3, 1024, [P, 2 * P], U8, "bytes01")
         quantise(words01, bytes01, grouped01)
-        words2 = on_pool(3, 4096, [P, P], U32, "words2")
-        bytes2 = on_pool(3, 5120, [P, P], U8, "bytes2")
+        product(words01, bytes01, 0, 2 * P, nc.scalar.copy)
+        words2 = after_gather(3, 4096, [P, P], U32, "words2")
+        bytes2 = after_gather(3, 5120, [P, P], U8, "bytes2")
         quantise(words2, bytes2, grouped2)
-
-        def product(bank, words, scale_bytes):
-            nc.tensor.matmul_mx(bank, lhsT=w_words[:].bitcast(FP8X4), lhsT_scale=w_bytes[:],
-                                rhs=words[:].bitcast(FP8X4), rhs_scale=scale_bytes[:], start=True, stop=True)
-
-        early = ps.tile([P, 3 * P], F32, name="early")
-        product(early[:, 0 : 2 * P], words01, bytes01)
-        product(early[:, 2 * P : 3 * P], words2, bytes2)
-        early_sb = sb.tile([P, 3 * P], F32, name="early_sb")
-        nc.scalar.copy(early_sb[:], early[:])
-        nc.sync.dma_start(out[:, 0 : 3 * P], early_sb[:])
-
+        product(words2, bytes2, 2 * P, P, nc.scalar.copy)
         words3 = sb.tile([P, P], U32, name="words3", align_bytes=64)
         bytes3 = sb.tile([P, P], U8, name="bytes3", align_bytes=64)
         quantise(words3, bytes3, grouped3)
-        last = ps.tile([P, P], F32, name="last")
-        product(last[:], words3, bytes3)
-        last_sb = sb.tile([P, P], F32, name="last_sb")
-        nc.vector.tensor_copy(last_sb[:], last[:])
-        nc.sync.dma_start(out[:, 3 * P : 4 * P], last_sb[:])
+        product(words3, bytes3, 3 * P, P, nc.vector.tensor_copy)

from contextlib import ExitStack

import concourse.mybir as mybir

F32 = mybir.dt.float32
BF16 = mybir.dt.bfloat16
I32 = mybir.dt.int32
U32 = mybir.dt.uint32
U16 = mybir.dt.uint16
U8 = mybir.dt.uint8
FP8X4 = mybir.dt.float8_e4m3fn_x4
ALU = mybir.AluOpType
ACT = mybir.ActivationFunctionType
AX = mybir.AxisListType

P = 128
D, E, T, I, Q, G = 512, 512, 2048, 512, 128, 64
PAGE = I // G
PACK = 4
QUADRANTS = 4
E_TILES = E // P
POOL_BYTES = 4 * T
RUN = 16
LN_FLOOR = 2.0**-64

FLOPS = 2 * Q * I * D + 2 * Q * I * E


def tile_attend_sharedpower_kernel(tc, query, keys_words, keys_scales, pw, slot_factor, vals, offs, out):
    nc = tc.nc
    with ExitStack() as ctx:
        sb = ctx.enter_context(tc.tile_pool(name="sb", bufs=1))
        placed = ctx.enter_context(tc.tile_pool(name="placed", bufs=1))
        ps = ctx.enter_context(tc.psum_pool(name="ps", bufs=1))

        vectors_at = (1 + E_TILES) * POOL_BYTES
        offsets = sb.tile([P, I // 16], U16, name="offsets")
        key_bytes = sb.tile([P, T], U8, name="key_bytes")
        q_raw = sb.tile([P, PACK, Q], F32, name="q_raw")
        zeros = [
            placed.tile([P, T], F32, name="zeros0", offset=0),
            placed.tile([P, E_TILES * T + 16], F32, name="zeros1", offset=POOL_BYTES),
        ]
        power = placed.tile([P, 1], F32, name="power", offset=vectors_at)
        factor_cols = placed.tile([P, PACK], F32, name="factor_cols", offset=vectors_at + 32)
        key_words = placed.tile([P, T], U32, name="key_words", offset=0)
        val_pool = [placed.tile([P, T], F32, name=f"val_pool{j}", offset=(1 + j) * POOL_BYTES) for j in range(E_TILES)]
        ident = sb.tile([P, P], F32, name="ident")

        def after_gather(j, at, shape, dtype, name):
            return placed.tile(shape, dtype, name=name, offset=(1 + j) * POOL_BYTES + at, align_bytes=64)

        def load_vals(j):
            nc.sync.dma_start(val_pool[j][:], vals[j * P : (j + 1) * P, :])

        nc.vector.memset(key_bytes[:].bitcast(I32), 0)
        half = P // 2
        for h in range(2):
            nc.gpsimd.memset(zeros[h][:, 0:half], 0.0)
            nc.gpsimd.affine_select(
                out=ident[:, h * half : (h + 1) * half],
                in_=zeros[h][:, 0:half],
                compare_op=ALU.not_equal,
                fill=1.0,
                base=-h * half,
                pattern=[[-1, half]],
                channel_multiplier=1,
            )

        nc.sync.dma_start(offsets[:], offs)
        nc.sync.dma_start(q_raw[:], query.rearrange("(p j) q -> p j q", j=PACK))
        for quad in range(QUADRANTS):
            queue = nc.sync if quad % 2 == 0 else nc.scalar
            queue.dma_start(
                key_bytes[32 * quad : 32 * quad + 4, :].bitcast(I32),
                keys_scales[0, 4 * quad : 4 * quad + 4, :].bitcast(I32),
            )
        nc.sync.dma_start(key_words[:].bitcast(I32), keys_words[0].rearrange("p n t -> p (n t)").bitcast(I32))
        load_vals(0)
        nc.sync.dma_start(power[:], pw)
        nc.sync.dma_start(factor_cols[:], slot_factor[0].rearrange("(p t) -> p t", t=PACK))
        for j in range(1, E_TILES):
            load_vals(j)

        def quantise(words, scale_bytes, grouped):
            nc.vector.quantize_mx(words[:].bitcast(FP8X4), scale_bytes[:], grouped[:])

        k_bytes = sb.tile([P, I], U8, name="k_bytes", align_bytes=64)
        k_words = sb.tile([P, I], U32, name="k_words", align_bytes=64)
        nc.vector.tensor_copy(k_bytes[:], key_bytes[:].indirect(offsets[:]))
        q_grouped = sb.tile([P, Q * PACK], BF16, name="q_grouped", align_bytes=64)
        nc.scalar.copy(q_grouped[:].rearrange("p (q j) -> p q j", j=PACK), q_raw[:].rearrange("p j q -> p q j"))
        q_words = sb.tile([P, Q], U32, name="q_words", align_bytes=64)
        q_bytes = sb.tile([P, Q], U8, name="q_bytes", align_bytes=64)
        quantise(q_words, q_bytes, q_grouped)
        scores = ps.tile([P, I], F32, name="scores")
        for h in range(2):
            slots = slice(h * I // 2, (h + 1) * I // 2)
            listed = offsets[:, slots.start // 16 : slots.stop // 16]
            nc.vector.tensor_copy(k_words[:, slots], key_words[:].indirect(listed))
            nc.tensor.matmul_mx(
                scores[:, slots],
                lhsT=q_words[:].bitcast(FP8X4),
                lhsT_scale=q_bytes[:],
                rhs=k_words[:, slots].bitcast(FP8X4),
                rhs_scale=k_bytes[:, slots],
                start=True,
                stop=True,
            )

        factor_rows = ps.tile([P, PACK, P], F32, name="factor_rows")
        for t in range(PACK):
            nc.tensor.transpose(factor_rows[:, t, :], factor_cols[:, t : t + 1].to_broadcast([P, P]), ident[:])

        neg_max = sb.tile([P, 1], F32, name="neg_max")
        nc.vector.tensor_reduce(neg_max[:], scores[:], AX.X, ALU.max, negate=True)
        row_sum = sb.tile([P, 1], F32, name="row_sum")
        exps = sb.tile([P, I], F32, name="exps")
        nc.scalar.activation(exps[:], scores[:], ACT.Exp, bias=neg_max[:], scale=1.0, accum_out=row_sum[:])
        row_log = sb.tile([P, 1], F32, name="row_log")
        nc.scalar.activation(row_log[:], row_sum[:], ACT.Ln)

        v_dealt = [sb.tile([P, I], BF16, name=f"v_dealt{j}") for j in range(E_TILES)]

        def gather_vals(j):
            nc.vector.tensor_copy(
                v_dealt[j][:].rearrange("p (u b y) -> p b u y", u=2, y=RUN), val_pool[j][:].indirect(offsets[:])
            )

        def turn(dealt, grouped, tag, bufs):
            pairs = dealt[:].bitcast(F32)
            turned = ps.tile([P, 2, P], F32, name="turned", tag=tag, bufs=bufs)
            for u in range(2):
                nc.tensor.transpose(turned[:, u, :], pairs[:, u * P : (u + 1) * P], ident[:])
            nc.scalar.copy(grouped.bitcast(F32).rearrange("p (c u) -> p c u", u=2), turned[:].rearrange("p u c -> p c u"))

        def turn_vals(j, grouped):
            turn(v_dealt[j], grouped, "v_turned", 2)

        gather_vals(0)
        page_sum = after_gather(0, 0, [P, G], F32, "page_sum")
        nc.vector.tensor_reduce(page_sum[:], exps[:].rearrange("p (g s) -> p g s", s=PAGE), AX.X, ALU.add)
        one_less_power = after_gather(0, 512, [P, 1], F32, "one_less_power")
        nc.vector.tensor_scalar(one_less_power[:], power[:], -1.0, 1.0, ALU.mult, ALU.add)
        neg_max_power = after_gather(0, 576, [P, 1], F32, "neg_max_power")
        nc.vector.tensor_tensor(neg_max_power[:], neg_max[:], power[:], ALU.mult)

        gather_vals(1)
        page_log = sb.tile([P, G], F32, name="page_log")
        nc.scalar.activation(page_log[:], page_sum[:], ACT.Ln, bias=LN_FLOOR, scale=1.0)
        page_term = after_gather(1, 0, [P, G], F32, "page_term")
        nc.vector.tensor_scalar(page_term[:], page_log[:], one_less_power[:], None, ALU.mult)
        row_term = after_gather(1, 256, [P, 1], F32, "row_term")
        nc.vector.tensor_tensor(row_term[:], neg_max_power[:], row_log[:], ALU.subtract)
        exponent = sb.tile([P, I], F32, name="exponent", tag="exponent_bytes", align_bytes=64)
        nc.vector.scalar_tensor_tensor(
            exponent[:].rearrange("p (g s) -> p g s", s=PAGE),
            scores[:].rearrange("p (g s) -> p g s", s=PAGE),
            power[:],
            page_term[:].unsqueeze(2).to_broadcast([P, G, PAGE]),
            ALU.mult,
            ALU.add,
        )

        gather_vals(2)
        shares = sb.tile([P, I], F32, name="shares")
        nc.scalar.activation(shares[:], exponent[:], ACT.Exp, bias=row_term[:], scale=1.0)
        grouped01 = sb.tile([P, 2 * I], BF16, name="grouped01", tag="exponent_bytes", align_bytes=64)
        turn_vals(0, grouped01[:, 0:I])
        turn_vals(1, grouped01[:, I : 2 * I])
        weights = after_gather(2, 4096, [P, I], BF16, "weights")
        nc.vector.tensor_tensor(
            weights[:].rearrange("p (u b n t) -> p b u n t", u=2, n=RUN // PACK, t=PACK),
            shares[:].rearrange("p (b u n t) -> p b u n t", u=2, n=RUN // PACK, t=PACK),
            factor_rows[:].rearrange("p t (b u n) -> p b u n t", u=2, n=RUN // PACK),
            ALU.mult,
        )
        grouped2 = sb.tile([P, I], BF16, name="grouped2", align_bytes=64)
        turn_vals(2, grouped2[:])
        w_grouped = sb.tile([P, I], BF16, name="w_grouped", align_bytes=64)
        turn(weights, w_grouped[:], "w_turned", 1)

        gather_vals(3)
        grouped3 = sb.tile([P, I], BF16, name="grouped3", align_bytes=64)
        turn_vals(3, grouped3[:])
        w_words = after_gather(3, 2048, [P, Q], U32, "w_words")
        w_bytes = after_gather(3, 3072, [P, Q], U8, "w_bytes")
        quantise(w_words, w_bytes, w_grouped)

        def product(words, scale_bytes, first, width, copy):
            bank = ps.tile([P, width], F32, name=f"bank{first}")
            nc.tensor.matmul_mx(
                bank[:],
                lhsT=w_words[:].bitcast(FP8X4),
                lhsT_scale=w_bytes[:],
                rhs=words[:].bitcast(FP8X4),
                rhs_scale=scale_bytes[:],
                start=True,
                stop=True,
            )
            staged = sb.tile([P, width], F32, name=f"staged{first}")
            copy(staged[:], bank[:])
            nc.sync.dma_start(out[:, first : first + width], staged[:])

        words01 = after_gather(3, 0, [P, 2 * P], U32, "words01")
        bytes01 = after_gather(3, 1024, [P, 2 * P], U8, "bytes01")
        quantise(words01, bytes01, grouped01)
        product(words01, bytes01, 0, 2 * P, nc.scalar.copy)
        words2 = after_gather(3, 4096, [P, P], U32, "words2")
        bytes2 = after_gather(3, 5120, [P, P], U8, "bytes2")
        quantise(words2, bytes2, grouped2)
        product(words2, bytes2, 2 * P, P, nc.scalar.copy)
        words3 = sb.tile([P, P], U32, name="words3", align_bytes=64)
        bytes3 = sb.tile([P, P], U8, name="bytes3", align_bytes=64)
        quantise(words3, bytes3, grouped3)
        product(words3, bytes3, 3 * P, P, nc.vector.tensor_copy)
